import numpy as np
import ml_dtypes


def mxq(x, axis, fmt="e4m3"):
    dtype, down = {"e4m3": (ml_dtypes.float8_e4m3fn, 7), "e5m2": (ml_dtypes.float8_e5m2, 14)}[fmt]
    v = np.moveaxis(np.asarray(x, np.float32).astype(ml_dtypes.bfloat16).astype(np.float64), axis, -1)
    blocks = v.reshape(v.shape[:-1] + (-1, 32))
    amax = np.abs(blocks).max(-1, keepdims=True)
    byte = np.maximum(np.where(amax > 0, np.frexp(amax)[1] - 1 + 127, 0) - down, 1)
    scale = np.exp2(byte - 127.0)
    codes = (blocks / scale).astype(np.float32).astype(dtype).astype(np.float64)
    return np.moveaxis((codes * scale).reshape(v.shape), -1, axis)


WIDE = False


def mx_kscale(k):
    if not WIDE:
        return np.ones(k)
    levels = np.array([10, -10, 5, -5, 0])
    if k % 512:
        return np.exp2(np.random.permutation(np.resize(levels, k // 32))).repeat(32)
    a = np.empty((k // 512, 16))
    for p in range(k // 512):
        a[p, :8] = np.random.permutation(np.resize(levels, 8))
        for g in range(8):
            far = levels[np.abs(levels - a[p, g]) >= 10]
            a[p, g + 8] = far[np.random.randint(len(far))]
    return np.exp2(a.ravel()).repeat(32)


def f64(x):
    return np.asarray(x).astype(np.float64)


def striped(idx):
    return np.tile(idx.reshape(-1, 16).T, (8, 1)).astype(np.uint16)


def unstriped(offs):
    return offs[:16].T.reshape(-1).astype(np.int64)


E2M1 = np.array([0.0, 0.5, 1.0, 1.5, 2.0, 3.0, 4.0, 6.0, -0.0, -0.5, -1.0, -1.5, -2.0, -3.0, -4.0, -6.0])


def pack_weight(w, fmt):
    k, n = w.shape
    w = f64(np.asarray(w, np.float32).astype(ml_dtypes.bfloat16)).reshape(k // 32, 32, n)
    amax = np.abs(w).max(1)
    if fmt == "e4m3":
        byte = np.frexp(amax)[1] - 1 + 127 - 7
    else:
        mant, ex = np.frexp(amax / 6.0)
        byte = np.where(mant > 0.5, ex, ex - 1) + 127
    byte = np.clip(np.where(amax > 0, byte, 1), 1, 254)
    scaled = (w * np.exp2(127.0 - byte)[:, None, :]).reshape(k, n).astype(np.float32)
    by_word = np.ascontiguousarray(scaled.reshape(k // 512, 128, 4, n).transpose(0, 1, 3, 2))
    if fmt == "e4m3":
        words = by_word.astype(ml_dtypes.float8_e4m3fn).view(np.uint8)
    else:
        c = by_word.astype(ml_dtypes.float4_e2m1fn).view(np.uint8) & 0xF
        words = (c[..., 0::2] | (c[..., 1::2] << 4)).reshape(k // 512, 128, 2 * n)
    return np.ascontiguousarray(words), np.ascontiguousarray(byte.astype(np.uint8).reshape(k // 512, 16, n))


def unpack_weight(words, scales, fmt):
    g, _, n = scales.shape
    words = np.ascontiguousarray(words).reshape(g, 128, n, -1)
    if fmt == "e4m3":
        vals = words.view(ml_dtypes.float8_e4m3fn).astype(np.float64)
    else:
        nib = np.empty((g, 128, n, 4), np.uint8)
        nib[..., 0::2] = words & 0xF
        nib[..., 1::2] = words >> 4
        vals = E2M1[nib]
    vals = vals * np.repeat(np.exp2(scales.astype(np.float64) - 127.0), 8, axis=1)[..., None]
    return vals.transpose(0, 1, 3, 2).reshape(g * 512, n)


def gelu(v):
    return 0.5 * v * (1.0 + np.tanh(np.sqrt(2.0 / np.pi) * (v + 0.044715 * v**3)))


K, T, S, S2 = 1024, 2048, 1024, 512


def setup_inputs():
    n = np.random.standard_normal
    s = mx_kscale(K)[:, None]
    d = {}
    d["tab_words"], d["tab_scales"] = pack_weight(n((K, T)) * s, "e4m3")
    d["offs"] = striped(np.random.permutation(T)[:S])
    d["offs2"] = striped(np.random.permutation(T)[:S2])
    d["w1"] = (n((K, K)) / K / s / s.T).astype(np.float32)
    d["w4_words"], d["w4_scales"] = pack_weight(1.5 * n((K, K)) / K ** 0.5 / s, "e2m1")
    d["gain"] = (1.2 * np.exp(0.3 * n(K)) * s[:, 0]).astype(np.float32)
    d["base"] = (0.6 * n(S2)).astype(np.float32)
    return d


def reference(tab_words, tab_scales, offs, offs2, w1, w4_words, w4_scales, gain, base):
    TW = unpack_weight(tab_words, tab_scales, "e4m3")
    v = TW[:, unstriped(offs)]
    v2 = TW[:, unstriped(offs2)]
    w4 = unpack_weight(w4_words, w4_scales, "e2m1")
    h = np.abs(mxq(f64(w1), 0, "e4m3").T @ v)
    hq = mxq(h, 0, "e4m3")
    b = np.tanh(w4.T @ v2) * f64(gain)[:, None]
    e1 = v2.T @ hq
    e2 = mxq(b, 0, "e4m3").T @ hq
    out = np.maximum(e1, e2) + f64(base)[:, None]
    return out

@@ -1,0 +1,237 @@
+from contextlib import ExitStack
+
+import concourse.mybir as mybir
+
+K, T, S, S2 = 1024, 2048, 1024, 512
+FLOPS = 2 * K * K * S + 2 * K * K * S2 + 2 * 2 * K * S2 * S
+
+F32 = mybir.dt.float32
+BF16 = mybir.dt.bfloat16
+I32 = mybir.dt.int32
+U32 = mybir.dt.uint32
+U16 = mybir.dt.uint16
+U8 = mybir.dt.uint8
+FP8X4 = mybir.dt.float8_e4m3fn_x4
+FP4X4 = mybir.dt.float4_e2m1fn_x4
+ACT = mybir.ActivationFunctionType
+ALU = mybir.AluOpType
+
+P = 128
+PACK = 4
+KP = P * PACK
+PASSES = K // KP
+BANK = 512
+
+
+def tile_list_feline_crossmatch_scores_kernel(
+    tc, tab_words, tab_scales, offs, offs2, w1, w4_words, w4_scales, gain, base, out
+):
+    nc = tc.nc
+    with ExitStack() as ctx:
+        keep = ctx.enter_context(tc.tile_pool(name="keep", bufs=1))
+        psum = ctx.enter_context(tc.psum_pool(name="psum", bufs=8))
+
+        def tile_in(pool, shape, dtype, name, bufs=1):
+            return pool.tile(shape, dtype, name=name, bufs=bufs, align_bytes=64)
+
+        def deal(dst, src):
+            nc.vector.tensor_copy(
+                dst.rearrange("p (b t q) -> p b t q", t=PACK, q=P),
+                src.rearrange("p (b q t) -> p b t q", t=PACK, q=P),
+            )
+
+        donors = tile_in(keep, [P, S // 16], U16, "donors")
+        recips = tile_in(keep, [P, S2 // 16], U16, "recips")
+        tab_s = tile_in(keep, [P, T], U8, "tab_s")
+        v2_s1 = tile_in(keep, [P, S2], U8, "v2_s1")
+        w4_w_raw = tile_in(keep, [P, PASSES, K], U16, "w4_w_raw")
+
+        w1_raw = {}
+
+        def load_w1(pool, a, b):
+            w1_raw[a, b] = tile_in(pool, [P, PACK, KP], F32, "w1_raw%d%d" % (a, b))
+            rows = w1[KP * a : KP * (a + 1), KP * b : KP * (b + 1)]
+            nc.sync.dma_start(w1_raw[a, b][:], rows.rearrange("(p j) c -> p j c", j=PACK))
+
+        def load_table(a):
+            nc.sync.dma_start(tab_w[a][:].bitcast(I32), tab_words[a].rearrange("p t i -> p (t i)").bitcast(I32))
+
+        nc.vector.memset(tab_s[:].bitcast(I32), 0)
+        with tc.tile_pool(name="warm_in", bufs=1) as left, tc.tile_pool(name="warm_out", bufs=1, side="right") as right:
+            warm_in = left.tile([P, 8], F32, name="warm_in")
+            warm_out = right.tile([P, 8], F32, name="warm_out")
+            nc.vector.memset(warm_in[:], 0.0)
+            nc.scalar.activation(warm_out[:], warm_in[:], ACT.Tanh)
+        nc.vector.memset(v2_s1[:].bitcast(I32), 0)
+
+        nc.sync.dma_start(recips[:], offs2)
+        nc.sync.dma_start(donors[:], offs)
+        nc.sync.dma_start(w4_w_raw[:].bitcast(I32), w4_words.rearrange("a p c -> p a c").bitcast(I32))
+        for q in range(4):
+            nc.sync.dma_start(
+                tab_s[32 * q : 32 * q + 8, :].bitcast(I32), tab_scales[:, 4 * q : 4 * q + 4, :].bitcast(I32)
+            )
+
+        main = ctx.enter_context(tc.tile_pool(name="main", bufs=1))
+        tab_w = [tile_in(main, [P, T], U32, "tab_w%d" % a) for a in range(PASSES)]
+        with tc.tile_pool(name="early", bufs=1, side="right") as early:
+            w4_s_raw = tile_in(early, [P, PASSES, K], U8, "w4_s_raw")
+            nc.gpsimd.memset(w4_s_raw[:].rearrange("p a c -> p (a c)").bitcast(I32), 0)
+            load_table(0)
+            for q in range(4):
+                nc.sync.dma_start(
+                    w4_s_raw[32 * q : 32 * q + 4, :, :].bitcast(I32),
+                    w4_scales[:, 4 * q : 4 * q + 4, :].rearrange("a r c -> r a c").bitcast(I32),
+                )
+            load_w1(main, 0, 0)
+            load_w1(main, 1, 0)
+            load_table(1)
+            gain_sb = tile_in(main, [P, PASSES, PACK], F32, "gain_sb")
+            nc.sync.dma_start(gain_sb[:], gain.rearrange("(b p t) -> p b t", p=P, t=PACK))
+
+            v2_s0 = tile_in(main, [P, S2], U8, "v2_s0")
+            w4_w = [tile_in(main, [P, K], U16, "w4_w%d" % a) for a in range(PASSES)]
+            w4_s = [tile_in(main, [P, K], U8, "w4_s%d" % a) for a in range(PASSES)]
+            for a in range(PASSES):
+                deal(w4_w[a][:], w4_w_raw[:, a, :])
+            nc.vector.tensor_copy(v2_s0[:], tab_s[:].indirect(recips[:]))
+            nc.sync.dma_start(v2_s1[0:100, :].bitcast(I32), v2_s0[4:104, :].bitcast(I32))
+            for a in range(PASSES):
+                deal(w4_s[a][:], w4_s_raw[:, a, :])
+
+        wide = ctx.enter_context(tc.tile_pool(name="wide", bufs=1, side="right"))
+        load_w1(wide, 0, 1)
+        load_w1(wide, 1, 1)
+        base_sb = tile_in(wide, [P, S2 // P], F32, "base_sb")
+        with nc.allow_non_contiguous_dma(reason="one base score for each partition"):
+            nc.sync.dma_start(base_sb[:], base.rearrange("(i p) -> p i", p=P))
+
+        v2_s = [v2_s0, v2_s1]
+        v2_w, v_s, v_w, w1_q, b_banks, b_q, h_q = {}, {}, {}, {}, {}, {}, {}
+
+        def gather_recipients(a):
+            v2_w[a] = tile_in(main, [P, S2], U32, "v2_w%d" % a)
+            nc.vector.tensor_copy(v2_w[a][:], tab_w[a][:].indirect(recips[:]))
+
+        def gather_donor_scales(jh):
+            v_s[jh] = tile_in(main, [P, BANK], U8, "v_s%d" % jh)
+            nc.vector.tensor_copy(v_s[jh][:], tab_s[:].indirect(donors[:, 32 * jh : 32 * (jh + 1)]))
+
+        def gather_donors(a, jh):
+            v_w[a, jh] = tile_in(main, [P, BANK], U32, "v_w%d%d" % (a, jh))
+            nc.vector.tensor_copy(v_w[a, jh][:], tab_w[a][:].indirect(donors[:, 32 * jh : 32 * (jh + 1)]))
+
+        def quantize(woven, name):
+            width = woven.shape[1] // PACK
+            codes = tile_in(main, [P, width], U32, name + "_w")
+            scales = tile_in(main, [P, width], U8, name + "_s")
+            nc.vector.quantize_mx(codes[:].bitcast(FP8X4), scales[:], woven)
+            return codes, scales
+
+        def cast_w1(a, b, copy):
+            woven = tile_in(main, [P, PACK * KP], BF16, "w1_bf", 3)
+            copy(
+                woven[:].rearrange("p (t m j) -> p m j t", t=PACK, j=PACK),
+                w1_raw[a, b][:].rearrange("p j (m t) -> p m j t", t=PACK),
+            )
+            w1_q[a, b] = quantize(woven[:], "w1_q%d%d" % (a, b))
+
+        def b_matmul(i):
+            rows = slice(P * i, P * (i + 1))
+            for b in range(PASSES):
+                bank = psum.tile([P, BANK], F32, name="bank")
+                for a in range(PASSES):
+                    for t in range(PACK):
+                        cols = slice(KP * b + P * t, KP * b + P * (t + 1))
+                        nc.tensor.matmul_mx(
+                            bank[:, P * t : P * (t + 1)],
+                            lhsT=w4_w[a][:, cols].bitcast(FP4X4),
+                            lhsT_scale=w4_s[a][:, cols],
+                            rhs=v2_w[a][:, rows].bitcast(FP8X4),
+                            rhs_scale=v2_s[a][:, rows],
+                            start=(a == 0 and t == 0),
+                            stop=(a == PASSES - 1 and t == PACK - 1),
+                        )
+                b_banks[b, i] = bank
+
+        def b_finish(i):
+            woven = tile_in(main, [P, PASSES, P, PACK], BF16, "b_bf", 3)
+            for b in range(PASSES):
+                bounded = tile_in(main, [P, P, PACK], F32, "bounded", 8)
+                nc.scalar.activation(bounded[:], b_banks[b, i][:].rearrange("p (t m) -> p m t", t=PACK), ACT.Tanh)
+                nc.vector.tensor_tensor(
+                    woven[:, b], bounded[:], gain_sb[:, b : b + 1, :].to_broadcast([P, P, PACK]), ALU.mult
+                )
+            b_q[i] = quantize(woven[:].rearrange("p b m t -> p (b m t)"), "b_q%d" % i)
+
+        def h_half(b, jh):
+            woven = tile_in(main, [P, BANK * PACK], BF16, "h_bf", 3)
+            for n in range(BANK // P):
+                bank = psum.tile([P, BANK], F32, name="bank")
+                cols = slice(P * n, P * (n + 1))
+                for a in range(PASSES):
+                    codes, scales = w1_q[a, b]
+                    for t in range(PACK):
+                        slot = slice(P * t, P * (t + 1))
+                        nc.tensor.matmul_mx(
+                            bank[:, slot],
+                            lhsT=codes[:, slot].bitcast(FP8X4),
+                            lhsT_scale=scales[:, slot],
+                            rhs=v_w[a, jh][:, cols].bitcast(FP8X4),
+                            rhs_scale=v_s[jh][4 * a : P, cols],
+                            start=(a == 0 and t == 0),
+                            stop=(a == PASSES - 1 and t == PACK - 1),
+                        )
+                nc.scalar.activation(
+                    woven[:, KP * n : KP * (n + 1)].rearrange("p (n t) -> p n t", t=PACK),
+                    bank[:].rearrange("p (t n) -> p n t", t=PACK),
+                    ACT.Abs,
+                )
+            h_q[b, jh] = quantize(woven[:], "h_q%d%d" % (b, jh))
+
+        def scores(i, jh):
+            rows = slice(P * i, P * (i + 1))
+            stored = [(v2_w[b][:, rows], v2_s[b][:, rows]) for b in range(PASSES)]
+            bounded = [tuple(part[:, P * b : P * (b + 1)] for part in b_q[i]) for b in range(PASSES)]
+            sums = []
+            for stationary in (stored, bounded):
+                bank = psum.tile([P, BANK], F32, name="bank")
+                for b in reversed(range(PASSES)):
+                    nc.tensor.matmul_mx(
+                        bank[:],
+                        lhsT=stationary[b][0].bitcast(FP8X4),
+                        lhsT_scale=stationary[b][1],
+                        rhs=h_q[b, jh][0][:].bitcast(FP8X4),
+                        rhs_scale=h_q[b, jh][1][:],
+                        start=(b == PASSES - 1),
+                        stop=(b == 0),
+                    )
+                sums.append(bank)
+            first = tile_in(main, [P, BANK], F32, "first", 3)
+            nc.scalar.activation(first[:], sums[0][:], ACT.Identity, bias=base_sb[:, i : i + 1])
+            result = tile_in(main, [P, BANK], F32, "result", 4)
+            nc.vector.scalar_tensor_tensor(result[:], sums[1][:], base_sb[:, i : i + 1], first[:], ALU.add, ALU.max)
+            nc.sync.dma_start(out[rows, BANK * jh : BANK * (jh + 1)], result[:])
+
+        for a in range(PASSES):
+            gather_recipients(a)
+        cast_w1(0, 0, nc.scalar.copy)
+        cast_w1(1, 0, nc.scalar.copy)
+        for jh in range(2):
+            gather_donor_scales(jh)
+        for jh in range(2):
+            for a in range(PASSES):
+                gather_donors(a, jh)
+        for i in range(S2 // P):
+            b_matmul(i)
+        cast_w1(0, 1, nc.vector.tensor_copy)
+        cast_w1(1, 1, nc.vector.tensor_copy)
+        for i in range(S2 // P - 1):
+            b_finish(i)
+        for b in range(PASSES):
+            for jh in range(2):
+                h_half(b, jh)
+        b_finish(S2 // P - 1)
+        for jh in range(2):
+            for i in range(S2 // P):
+                scores(i, jh)

@@ -75,13 +75,12 @@ def tile_list_feline_crossmatch_scores_kernel(
         main = ctx.enter_context(tc.tile_pool(name="main", bufs=1))
         tab_w = [tile_in(main, [P, T], U32, "tab_w%d" % a) for a in range(PASSES)]
         with tc.tile_pool(name="early", bufs=1, side="right") as early:
-            w4_s_raw = tile_in(early, [P, PASSES, K], U8, "w4_s_raw")
-            nc.gpsimd.memset(w4_s_raw[:].rearrange("p a c -> p (a c)").bitcast(I32), 0)
+            w4_s_raw = tile_in(early, [P, K], U8, "w4_s_raw")
+            nc.gpsimd.memset(w4_s_raw[:].bitcast(I32), 0)
             load_table(0)
             for q in range(4):
                 nc.sync.dma_start(
-                    w4_s_raw[32 * q : 32 * q + 4, :, :].bitcast(I32),
-                    w4_scales[:, 4 * q : 4 * q + 4, :].rearrange("a r c -> r a c").bitcast(I32),
+                    w4_s_raw[32 * q : 32 * q + 8, :].bitcast(I32), w4_scales[:, 4 * q : 4 * q + 4, :].bitcast(I32)
                 )
             load_w1(main, 0, 0)
             load_w1(main, 1, 0)
@@ -96,8 +95,9 @@ def tile_list_feline_crossmatch_scores_kernel(
                 deal(w4_w[a][:], w4_w_raw[:, a, :])
             nc.vector.tensor_copy(v2_s0[:], tab_s[:].indirect(recips[:]))
             nc.sync.dma_start(v2_s1[0:100, :].bitcast(I32), v2_s0[4:104, :].bitcast(I32))
-            for a in range(PASSES):
-                deal(w4_s[a][:], w4_s_raw[:, a, :])
+            nc.gpsimd.memset(w4_s[1][:].bitcast(I32), 0)
+            deal(w4_s[0][:], w4_s_raw[:])
+            nc.sync.dma_start(w4_s[1][0:100, :].bitcast(I32), w4_s[0][4:104, :].bitcast(I32))
 
         wide = ctx.enter_context(tc.tile_pool(name="wide", bufs=1, side="right"))
         load_w1(wide, 0, 1)
@@ -131,8 +131,8 @@ def tile_list_feline_crossmatch_scores_kernel(
         def cast_w1(a, b, copy):
             woven = tile_in(main, [P, PACK * KP], BF16, "w1_bf", 3)
             copy(
-                woven[:].rearrange("p (t m j) -> p m j t", t=PACK, j=PACK),
-                w1_raw[a, b][:].rearrange("p j (m t) -> p m j t", t=PACK),
+                woven[:].rearrange("p (u e m j) -> p u m e j", u=2, e=2, j=PACK),
+                w1_raw[a, b][:].rearrange("p j (m u e) -> p u m e j", u=2, e=2),
             )
             w1_q[a, b] = quantize(woven[:], "w1_q%d%d" % (a, b))
 
@@ -189,8 +189,9 @@ def tile_list_feline_crossmatch_scores_kernel(
                 )
             h_q[b, jh] = quantize(woven[:], "h_q%d%d" % (b, jh))
 
-        def scores(i, jh):
+        def scores(i, jh, lo, width):
             rows = slice(P * i, P * (i + 1))
+            cols = slice(lo, lo + width)
             stored = [(v2_w[b][:, rows], v2_s[b][:, rows]) for b in range(PASSES)]
             bounded = [tuple(part[:, P * b : P * (b + 1)] for part in b_q[i]) for b in range(PASSES)]
             sums = []
@@ -198,20 +199,20 @@ def tile_list_feline_crossmatch_scores_kernel(
                 bank = psum.tile([P, BANK], F32, name="bank")
                 for b in reversed(range(PASSES)):
                     nc.tensor.matmul_mx(
-                        bank[:],
+                        bank[:, 0:width],
                         lhsT=stationary[b][0].bitcast(FP8X4),
                         lhsT_scale=stationary[b][1],
-                        rhs=h_q[b, jh][0][:].bitcast(FP8X4),
-                        rhs_scale=h_q[b, jh][1][:],
+                        rhs=h_q[b, jh][0][:, cols].bitcast(FP8X4),
+                        rhs_scale=h_q[b, jh][1][:, cols],
                         start=(b == PASSES - 1),
                         stop=(b == 0),
                     )
-                sums.append(bank)
-            first = tile_in(main, [P, BANK], F32, "first", 3)
-            nc.scalar.activation(first[:], sums[0][:], ACT.Identity, bias=base_sb[:, i : i + 1])
-            result = tile_in(main, [P, BANK], F32, "result", 4)
-            nc.vector.scalar_tensor_tensor(result[:], sums[1][:], base_sb[:, i : i + 1], first[:], ALU.add, ALU.max)
-            nc.sync.dma_start(out[rows, BANK * jh : BANK * (jh + 1)], result[:])
+                sums.append(bank[:, 0:width])
+            first = tile_in(main, [P, width], F32, "first", 3)
+            nc.scalar.activation(first[:], sums[0], ACT.Identity, bias=base_sb[:, i : i + 1])
+            result = tile_in(main, [P, width], F32, "result", 4)
+            nc.vector.scalar_tensor_tensor(result[:], sums[1], base_sb[:, i : i + 1], first[:], ALU.add, ALU.max)
+            nc.sync.dma_start(out[rows, BANK * jh + lo : BANK * jh + lo + width], result[:])
 
         for a in range(PASSES):
             gather_recipients(a)
@@ -234,4 +235,7 @@ def tile_list_feline_crossmatch_scores_kernel(
         b_finish(S2 // P - 1)
         for jh in range(2):
             for i in range(S2 // P):
-                scores(i, jh)
+                last = jh == 1 and i == S2 // P - 1
+                width = BANK // 2 if last else BANK
+                for lo in range(0, BANK, width):
+                    scores(i, jh, lo, width)

@@ -131,8 +131,8 @@ def tile_list_feline_crossmatch_scores_kernel(
         def cast_w1(a, b, copy):
             woven = tile_in(main, [P, PACK * KP], BF16, "w1_bf", 3)
             copy(
-                woven[:].rearrange("p (u e m j) -> p u m e j", u=2, e=2, j=PACK),
-                w1_raw[a, b][:].rearrange("p j (m u e) -> p u m e j", u=2, e=2),
+                woven[:].rearrange("p (t m j) -> p m t j", t=PACK, j=PACK),
+                w1_raw[a, b][:].rearrange("p j (m t) -> p m t j", t=PACK),
             )
             w1_q[a, b] = quantize(woven[:], "w1_q%d%d" % (a, b))
 

@@ -57,12 +57,10 @@ def tile_list_feline_crossmatch_scores_kernel(
             nc.sync.dma_start(tab_w[a][:].bitcast(I32), tab_words[a].rearrange("p t i -> p (t i)").bitcast(I32))
 
         nc.vector.memset(tab_s[:].bitcast(I32), 0)
-        with tc.tile_pool(name="warm_in", bufs=1) as left, tc.tile_pool(name="warm_out", bufs=1, side="right") as right:
-            warm_in = left.tile([P, 8], F32, name="warm_in")
-            warm_out = right.tile([P, 8], F32, name="warm_out")
-            nc.vector.memset(warm_in[:], 0.0)
-            nc.scalar.activation(warm_out[:], warm_in[:], ACT.Tanh)
-        nc.vector.memset(v2_s1[:].bitcast(I32), 0)
+        warm = tile_in(keep, [P, 8], F32, "warm")
+        nc.gpsimd.memset(warm[:, 0:4], 0.0)
+        nc.scalar.activation(warm[:, 4:8], warm[:, 0:4], ACT.Tanh)
+        nc.gpsimd.memset(v2_s1[:].bitcast(I32), 0)
 
         nc.sync.dma_start(recips[:], offs2)
         nc.sync.dma_start(donors[:], offs)
@@ -72,11 +70,14 @@ def tile_list_feline_crossmatch_scores_kernel(
                 tab_s[32 * q : 32 * q + 8, :].bitcast(I32), tab_scales[:, 4 * q : 4 * q + 4, :].bitcast(I32)
             )
 
-        main = ctx.enter_context(tc.tile_pool(name="main", bufs=1))
-        tab_w = [tile_in(main, [P, T], U32, "tab_w%d" % a) for a in range(PASSES)]
         with tc.tile_pool(name="early", bufs=1, side="right") as early:
             w4_s_raw = tile_in(early, [P, K], U8, "w4_s_raw")
-            nc.gpsimd.memset(w4_s_raw[:].bitcast(I32), 0)
+            with tc.tile_pool(name="head", bufs=1) as head:
+                zeros = tile_in(head, [P, K // 4], I32, "zeros")
+                nc.vector.memset(zeros[:], 0)
+                nc.vector.tensor_copy(w4_s_raw[:].bitcast(I32), zeros[:])
+            main = ctx.enter_context(tc.tile_pool(name="main", bufs=1))
+            tab_w = [tile_in(main, [P, T], U32, "tab_w%d" % a) for a in range(PASSES)]
             load_table(0)
             for q in range(4):
                 nc.sync.dma_start(
@@ -118,7 +119,8 @@ def tile_list_feline_crossmatch_scores_kernel(
             nc.vector.tensor_copy(v_s[jh][:], tab_s[:].indirect(donors[:, 32 * jh : 32 * (jh + 1)]))
 
         def gather_donors(a, jh):
-            v_w[a, jh] = tile_in(main, [P, BANK], U32, "v_w%d%d" % (a, jh))
+            name = "v_w%d%d" % (a, jh)
+            v_w[a, jh] = tile_in(wide, [P, BANK], U32, name)
             nc.vector.tensor_copy(v_w[a, jh][:], tab_w[a][:].indirect(donors[:, 32 * jh : 32 * (jh + 1)]))
 
         def quantize(woven, name):
@@ -131,38 +133,39 @@ def tile_list_feline_crossmatch_scores_kernel(
         def cast_w1(a, b, copy):
             woven = tile_in(main, [P, PACK * KP], BF16, "w1_bf", 3)
             copy(
-                woven[:].rearrange("p (t m j) -> p m t j", t=PACK, j=PACK),
-                w1_raw[a, b][:].rearrange("p j (m t) -> p m t j", t=PACK),
+                woven[:].rearrange("p (t m j) -> p m j t", t=PACK, j=PACK),
+                w1_raw[a, b][:].rearrange("p j (m t) -> p m j t", t=PACK),
             )
             w1_q[a, b] = quantize(woven[:], "w1_q%d%d" % (a, b))
 
-        def b_matmul(i):
-            rows = slice(P * i, P * (i + 1))
-            for b in range(PASSES):
+        def b_matmul(b):
+            for t in range(PACK):
                 bank = psum.tile([P, BANK], F32, name="bank")
+                cols = slice(KP * b + P * t, KP * b + P * (t + 1))
                 for a in range(PASSES):
-                    for t in range(PACK):
-                        cols = slice(KP * b + P * t, KP * b + P * (t + 1))
-                        nc.tensor.matmul_mx(
-                            bank[:, P * t : P * (t + 1)],
-                            lhsT=w4_w[a][:, cols].bitcast(FP4X4),
-                            lhsT_scale=w4_s[a][:, cols],
-                            rhs=v2_w[a][:, rows].bitcast(FP8X4),
-                            rhs_scale=v2_s[a][:, rows],
-                            start=(a == 0 and t == 0),
-                            stop=(a == PASSES - 1 and t == PACK - 1),
-                        )
-                b_banks[b, i] = bank
+                    nc.tensor.matmul_mx(
+                        bank[:],
+                        lhsT=w4_w[a][:, cols].bitcast(FP4X4),
+                        lhsT_scale=w4_s[a][:, cols],
+                        rhs=v2_w[a][:].bitcast(FP8X4),
+                        rhs_scale=v2_s[a][:],
+                        start=(a == 0),
+                        stop=(a == PASSES - 1),
+                    )
+                b_banks[b, t] = bank
 
-        def b_finish(i):
-            woven = tile_in(main, [P, PASSES, P, PACK], BF16, "b_bf", 3)
-            for b in range(PASSES):
-                bounded = tile_in(main, [P, P, PACK], F32, "bounded", 8)
-                nc.scalar.activation(bounded[:], b_banks[b, i][:].rearrange("p (t m) -> p m t", t=PACK), ACT.Tanh)
-                nc.vector.tensor_tensor(
-                    woven[:, b], bounded[:], gain_sb[:, b : b + 1, :].to_broadcast([P, P, PACK]), ALU.mult
-                )
-            b_q[i] = quantize(woven[:].rearrange("p b m t -> p (b m t)"), "b_q%d" % i)
+        def b_finish(b):
+            slots = tile_in(main, [P, PACK, S2], BF16, "b_slots", 2)
+            for t in range(PACK):
+                bounded = tile_in(main, [P, S2], F32, "bounded", 8)
+                nc.scalar.activation(bounded[:], b_banks[b, t][:], ACT.Tanh)
+                nc.vector.tensor_scalar_mul(slots[:, t, :], bounded[:], gain_sb[:, b, t : t + 1])
+            woven = tile_in(main, [P, S2 * PACK], BF16, "b_bf", 2)
+            nc.vector.tensor_copy(
+                woven[:].rearrange("p (c i t) -> p c t i", i=4, t=PACK),
+                slots[:].rearrange("p t (c i) -> p c t i", i=4),
+            )
+            b_q[b] = quantize(woven[:], "b_q%d" % b)
 
         def h_half(b, jh):
             woven = tile_in(main, [P, BANK * PACK], BF16, "h_bf", 3)
@@ -193,7 +196,7 @@ def tile_list_feline_crossmatch_scores_kernel(
             rows = slice(P * i, P * (i + 1))
             cols = slice(lo, lo + width)
             stored = [(v2_w[b][:, rows], v2_s[b][:, rows]) for b in range(PASSES)]
-            bounded = [tuple(part[:, P * b : P * (b + 1)] for part in b_q[i]) for b in range(PASSES)]
+            bounded = [tuple(part[:, rows] for part in b_q[b]) for b in range(PASSES)]
             sums = []
             for stationary in (stored, bounded):
                 bank = psum.tile([P, BANK], F32, name="bank")
@@ -223,16 +226,15 @@ def tile_list_feline_crossmatch_scores_kernel(
         for jh in range(2):
             for a in range(PASSES):
                 gather_donors(a, jh)
-        for i in range(S2 // P):
-            b_matmul(i)
+        for b in range(PASSES):
+            b_matmul(b)
         cast_w1(0, 1, nc.vector.tensor_copy)
         cast_w1(1, 1, nc.vector.tensor_copy)
-        for i in range(S2 // P - 1):
-            b_finish(i)
+        for b in range(PASSES):
+            b_finish(b)
         for b in range(PASSES):
             for jh in range(2):
                 h_half(b, jh)
-        b_finish(S2 // P - 1)
         for jh in range(2):
             for i in range(S2 // P):
                 last = jh == 1 and i == S2 // P - 1

@@ -57,9 +57,6 @@ def tile_list_feline_crossmatch_scores_kernel(
             nc.sync.dma_start(tab_w[a][:].bitcast(I32), tab_words[a].rearrange("p t i -> p (t i)").bitcast(I32))
 
         nc.vector.memset(tab_s[:].bitcast(I32), 0)
-        warm = tile_in(keep, [P, 8], F32, "warm")
-        nc.gpsimd.memset(warm[:, 0:4], 0.0)
-        nc.scalar.activation(warm[:, 4:8], warm[:, 0:4], ACT.Tanh)
         nc.gpsimd.memset(v2_s1[:].bitcast(I32), 0)
 
         nc.sync.dma_start(recips[:], offs2)

from contextlib import ExitStack

import concourse.mybir as mybir

K, T, S, S2 = 1024, 2048, 1024, 512
FLOPS = 2 * K * K * S + 2 * K * K * S2 + 2 * 2 * K * S2 * S

F32 = mybir.dt.float32
BF16 = mybir.dt.bfloat16
I32 = mybir.dt.int32
U32 = mybir.dt.uint32
U16 = mybir.dt.uint16
U8 = mybir.dt.uint8
FP8X4 = mybir.dt.float8_e4m3fn_x4
FP4X4 = mybir.dt.float4_e2m1fn_x4
ACT = mybir.ActivationFunctionType
ALU = mybir.AluOpType

P = 128
PACK = 4
KP = P * PACK
PASSES = K // KP
BANK = 512


def tile_list_feline_crossmatch_scores_kernel(
    tc, tab_words, tab_scales, offs, offs2, w1, w4_words, w4_scales, gain, base, out
):
    nc = tc.nc
    with ExitStack() as ctx:
        keep = ctx.enter_context(tc.tile_pool(name="keep", bufs=1))
        psum = ctx.enter_context(tc.psum_pool(name="psum", bufs=8))

        def tile_in(pool, shape, dtype, name, bufs=1):
            return pool.tile(shape, dtype, name=name, bufs=bufs, align_bytes=64)

        def deal(dst, src):
            nc.vector.tensor_copy(
                dst.rearrange("p (b t q) -> p b t q", t=PACK, q=P),
                src.rearrange("p (b q t) -> p b t q", t=PACK, q=P),
            )

        donors = tile_in(keep, [P, S // 16], U16, "donors")
        recips = tile_in(keep, [P, S2 // 16], U16, "recips")
        tab_s = tile_in(keep, [P, T], U8, "tab_s")
        v2_s1 = tile_in(keep, [P, S2], U8, "v2_s1")
        w4_w_raw = tile_in(keep, [P, PASSES, K], U16, "w4_w_raw")

        w1_raw = {}

        def load_w1(pool, a, b):
            w1_raw[a, b] = tile_in(pool, [P, PACK, KP], F32, "w1_raw%d%d" % (a, b))
            rows = w1[KP * a : KP * (a + 1), KP * b : KP * (b + 1)]
            nc.sync.dma_start(w1_raw[a, b][:], rows.rearrange("(p j) c -> p j c", j=PACK))

        def load_table(a):
            nc.sync.dma_start(tab_w[a][:].bitcast(I32), tab_words[a].rearrange("p t i -> p (t i)").bitcast(I32))

        nc.vector.memset(tab_s[:].bitcast(I32), 0)
        nc.gpsimd.memset(v2_s1[:].bitcast(I32), 0)

        nc.sync.dma_start(recips[:], offs2)
        nc.sync.dma_start(donors[:], offs)
        nc.sync.dma_start(w4_w_raw[:].bitcast(I32), w4_words.rearrange("a p c -> p a c").bitcast(I32))
        for q in range(4):
            nc.sync.dma_start(
                tab_s[32 * q : 32 * q + 8, :].bitcast(I32), tab_scales[:, 4 * q : 4 * q + 4, :].bitcast(I32)
            )

        with tc.tile_pool(name="early", bufs=1, side="right") as early:
            w4_s_raw = tile_in(early, [P, K], U8, "w4_s_raw")
            with tc.tile_pool(name="head", bufs=1) as head:
                zeros = tile_in(head, [P, K // 4], I32, "zeros")
                nc.vector.memset(zeros[:], 0)
                nc.vector.tensor_copy(w4_s_raw[:].bitcast(I32), zeros[:])
            main = ctx.enter_context(tc.tile_pool(name="main", bufs=1))
            tab_w = [tile_in(main, [P, T], U32, "tab_w%d" % a) for a in range(PASSES)]
            load_table(0)
            for q in range(4):
                nc.sync.dma_start(
                    w4_s_raw[32 * q : 32 * q + 8, :].bitcast(I32), w4_scales[:, 4 * q : 4 * q + 4, :].bitcast(I32)
                )
            load_w1(main, 0, 0)
            load_w1(main, 1, 0)
            load_table(1)
            gain_sb = tile_in(main, [P, PASSES, PACK], F32, "gain_sb")
            nc.sync.dma_start(gain_sb[:], gain.rearrange("(b p t) -> p b t", p=P, t=PACK))

            v2_s0 = tile_in(main, [P, S2], U8, "v2_s0")
            w4_w = [tile_in(main, [P, K], U16, "w4_w%d" % a) for a in range(PASSES)]
            w4_s = [tile_in(main, [P, K], U8, "w4_s%d" % a) for a in range(PASSES)]
            for a in range(PASSES):
                deal(w4_w[a][:], w4_w_raw[:, a, :])
            nc.vector.tensor_copy(v2_s0[:], tab_s[:].indirect(recips[:]))
            nc.sync.dma_start(v2_s1[0:100, :].bitcast(I32), v2_s0[4:104, :].bitcast(I32))
            nc.gpsimd.memset(w4_s[1][:].bitcast(I32), 0)
            deal(w4_s[0][:], w4_s_raw[:])
            nc.sync.dma_start(w4_s[1][0:100, :].bitcast(I32), w4_s[0][4:104, :].bitcast(I32))

        wide = ctx.enter_context(tc.tile_pool(name="wide", bufs=1, side="right"))
        load_w1(wide, 0, 1)
        load_w1(wide, 1, 1)
        base_sb = tile_in(wide, [P, S2 // P], F32, "base_sb")
        with nc.allow_non_contiguous_dma(reason="one base score for each partition"):
            nc.sync.dma_start(base_sb[:], base.rearrange("(i p) -> p i", p=P))

        v2_s = [v2_s0, v2_s1]
        v2_w, v_s, v_w, w1_q, b_banks, b_q, h_q = {}, {}, {}, {}, {}, {}, {}

        def gather_recipients(a):
            v2_w[a] = tile_in(main, [P, S2], U32, "v2_w%d" % a)
            nc.vector.tensor_copy(v2_w[a][:], tab_w[a][:].indirect(recips[:]))

        def gather_donor_scales(jh):
            v_s[jh] = tile_in(main, [P, BANK], U8, "v_s%d" % jh)
            nc.vector.tensor_copy(v_s[jh][:], tab_s[:].indirect(donors[:, 32 * jh : 32 * (jh + 1)]))

        def gather_donors(a, jh):
            name = "v_w%d%d" % (a, jh)
            v_w[a, jh] = tile_in(wide, [P, BANK], U32, name)
            nc.vector.tensor_copy(v_w[a, jh][:], tab_w[a][:].indirect(donors[:, 32 * jh : 32 * (jh + 1)]))

        def quantize(woven, name):
            width = woven.shape[1] // PACK
            codes = tile_in(main, [P, width], U32, name + "_w")
            scales = tile_in(main, [P, width], U8, name + "_s")
            nc.vector.quantize_mx(codes[:].bitcast(FP8X4), scales[:], woven)
            return codes, scales

        def cast_w1(a, b, copy):
            woven = tile_in(main, [P, PACK * KP], BF16, "w1_bf", 3)
            copy(
                woven[:].rearrange("p (t m j) -> p m j t", t=PACK, j=PACK),
                w1_raw[a, b][:].rearrange("p j (m t) -> p m j t", t=PACK),
            )
            w1_q[a, b] = quantize(woven[:], "w1_q%d%d" % (a, b))

        def b_matmul(b):
            for t in range(PACK):
                bank = psum.tile([P, BANK], F32, name="bank")
                cols = slice(KP * b + P * t, KP * b + P * (t + 1))
                for a in range(PASSES):
                    nc.tensor.matmul_mx(
                        bank[:],
                        lhsT=w4_w[a][:, cols].bitcast(FP4X4),
                        lhsT_scale=w4_s[a][:, cols],
                        rhs=v2_w[a][:].bitcast(FP8X4),
                        rhs_scale=v2_s[a][:],
                        start=(a == 0),
                        stop=(a == PASSES - 1),
                    )
                b_banks[b, t] = bank

        def b_finish(b):
            slots = tile_in(main, [P, PACK, S2], BF16, "b_slots", 2)
            for t in range(PACK):
                bounded = tile_in(main, [P, S2], F32, "bounded", 8)
                nc.scalar.activation(bounded[:], b_banks[b, t][:], ACT.Tanh)
                nc.vector.tensor_scalar_mul(slots[:, t, :], bounded[:], gain_sb[:, b, t : t + 1])
            woven = tile_in(main, [P, S2 * PACK], BF16, "b_bf", 2)
            nc.vector.tensor_copy(
                woven[:].rearrange("p (c i t) -> p c t i", i=4, t=PACK),
                slots[:].rearrange("p t (c i) -> p c t i", i=4),
            )
            b_q[b] = quantize(woven[:], "b_q%d" % b)

        def h_half(b, jh):
            woven = tile_in(main, [P, BANK * PACK], BF16, "h_bf", 3)
            for n in range(BANK // P):
                bank = psum.tile([P, BANK], F32, name="bank")
                cols = slice(P * n, P * (n + 1))
                for a in range(PASSES):
                    codes, scales = w1_q[a, b]
                    for t in range(PACK):
                        slot = slice(P * t, P * (t + 1))
                        nc.tensor.matmul_mx(
                            bank[:, slot],
                            lhsT=codes[:, slot].bitcast(FP8X4),
                            lhsT_scale=scales[:, slot],
                            rhs=v_w[a, jh][:, cols].bitcast(FP8X4),
                            rhs_scale=v_s[jh][4 * a : P, cols],
                            start=(a == 0 and t == 0),
                            stop=(a == PASSES - 1 and t == PACK - 1),
                        )
                nc.scalar.activation(
                    woven[:, KP * n : KP * (n + 1)].rearrange("p (n t) -> p n t", t=PACK),
                    bank[:].rearrange("p (t n) -> p n t", t=PACK),
                    ACT.Abs,
                )
            h_q[b, jh] = quantize(woven[:], "h_q%d%d" % (b, jh))

        def scores(i, jh, lo, width):
            rows = slice(P * i, P * (i + 1))
            cols = slice(lo, lo + width)
            stored = [(v2_w[b][:, rows], v2_s[b][:, rows]) for b in range(PASSES)]
            bounded = [tuple(part[:, rows] for part in b_q[b]) for b in range(PASSES)]
            sums = []
            for stationary in (stored, bounded):
                bank = psum.tile([P, BANK], F32, name="bank")
                for b in reversed(range(PASSES)):
                    nc.tensor.matmul_mx(
                        bank[:, 0:width],
                        lhsT=stationary[b][0].bitcast(FP8X4),
                        lhsT_scale=stationary[b][1],
                        rhs=h_q[b, jh][0][:, cols].bitcast(FP8X4),
                        rhs_scale=h_q[b, jh][1][:, cols],
                        start=(b == PASSES - 1),
                        stop=(b == 0),
                    )
                sums.append(bank[:, 0:width])
            first = tile_in(main, [P, width], F32, "first", 3)
            nc.scalar.activation(first[:], sums[0], ACT.Identity, bias=base_sb[:, i : i + 1])
            result = tile_in(main, [P, width], F32, "result", 4)
            nc.vector.scalar_tensor_tensor(result[:], sums[1], base_sb[:, i : i + 1], first[:], ALU.add, ALU.max)
            nc.sync.dma_start(out[rows, BANK * jh + lo : BANK * jh + lo + width], result[:])

        for a in range(PASSES):
            gather_recipients(a)
        cast_w1(0, 0, nc.scalar.copy)
        cast_w1(1, 0, nc.scalar.copy)
        for jh in range(2):
            gather_donor_scales(jh)
        for jh in range(2):
            for a in range(PASSES):
                gather_donors(a, jh)
        for b in range(PASSES):
            b_matmul(b)
        cast_w1(0, 1, nc.vector.tensor_copy)
        cast_w1(1, 1, nc.vector.tensor_copy)
        for b in range(PASSES):
            b_finish(b)
        for b in range(PASSES):
            for jh in range(2):
                h_half(b, jh)
        for jh in range(2):
            for i in range(S2 // P):
                last = jh == 1 and i == S2 // P - 1
                width = BANK // 2 if last else BANK
                for lo in range(0, BANK, width):
                    scores(i, jh, lo, width)
